import numpy as np
import ml_dtypes


def mxq(x, axis, fmt="e4m3"):
    dtype, down = {"e4m3": (ml_dtypes.float8_e4m3fn, 7), "e5m2": (ml_dtypes.float8_e5m2, 14)}[fmt]
    v = np.moveaxis(np.asarray(x, np.float32).astype(ml_dtypes.bfloat16).astype(np.float64), axis, -1)
    blocks = v.reshape(v.shape[:-1] + (-1, 32))
    amax = np.abs(blocks).max(-1, keepdims=True)
    byte = np.maximum(np.where(amax > 0, np.frexp(amax)[1] - 1 + 127, 0) - down, 1)
    scale = np.exp2(byte - 127.0)
    codes = (blocks / scale).astype(np.float32).astype(dtype).astype(np.float64)
    return np.moveaxis((codes * scale).reshape(v.shape), -1, axis)


WIDE = False


def mx_kscale(k):
    if not WIDE:
        return np.ones(k)
    levels = np.array([10, -10, 5, -5, 0])
    if k % 512:
        return np.exp2(np.random.permutation(np.resize(levels, k // 32))).repeat(32)
    a = np.empty((k // 512, 16))
    for p in range(k // 512):
        a[p, :8] = np.random.permutation(np.resize(levels, 8))
        for g in range(8):
            far = levels[np.abs(levels - a[p, g]) >= 10]
            a[p, g + 8] = far[np.random.randint(len(far))]
    return np.exp2(a.ravel()).repeat(32)


def f64(x):
    return np.asarray(x).astype(np.float64)


def striped(idx):
    return np.tile(np.asarray(idx).reshape(-1, 16).T, (8, 1)).astype(np.uint16)


def unstriped(offs):
    return offs[:16].T.reshape(-1).astype(np.int64)


def striped8(idx):
    return np.asarray(idx).reshape(8, -1, 16).transpose(0, 2, 1).reshape(128, -1).astype(np.uint16)


def unstriped8(offs):
    return offs.reshape(8, 16, -1).transpose(0, 2, 1).reshape(8, -1).astype(np.int64)


def pick8(x, idx, run):
    r = np.arange(len(x))
    return x[r[:, None], idx[r % (8 * run) // run]]


E2M1 = np.array([0.0, 0.5, 1.0, 1.5, 2.0, 3.0, 4.0, 6.0, -0.0, -0.5, -1.0, -1.5, -2.0, -3.0, -4.0, -6.0])


def pack_weight(w, fmt):
    k, n = w.shape
    w = f64(np.asarray(w, np.float32).astype(ml_dtypes.bfloat16)).reshape(k // 32, 32, n)
    amax = np.abs(w).max(1)
    if fmt == "e4m3":
        byte = np.frexp(amax)[1] - 1 + 127 - 7
    else:
        mant, ex = np.frexp(amax / 6.0)
        byte = np.where(mant > 0.5, ex, ex - 1) + 127
    byte = np.clip(np.where(amax > 0, byte, 1), 1, 254)
    scaled = (w * np.exp2(127.0 - byte)[:, None, :]).reshape(k, n).astype(np.float32)
    by_word = np.ascontiguousarray(scaled.reshape(k // 512, 128, 4, n).transpose(0, 1, 3, 2))
    if fmt == "e4m3":
        words = by_word.astype(ml_dtypes.float8_e4m3fn).view(np.uint8)
    else:
        c = by_word.astype(ml_dtypes.float4_e2m1fn).view(np.uint8) & 0xF
        words = (c[..., 0::2] | (c[..., 1::2] << 4)).reshape(k // 512, 128, 2 * n)
    return np.ascontiguousarray(words), np.ascontiguousarray(byte.astype(np.uint8).reshape(k // 512, 16, n))


def unpack_weight(words, scales, fmt):
    g, _, n = scales.shape
    words = np.ascontiguousarray(words).reshape(g, 128, n, -1)
    if fmt == "e4m3":
        vals = words.view(ml_dtypes.float8_e4m3fn).astype(np.float64)
    else:
        nib = np.empty((g, 128, n, 4), np.uint8)
        nib[..., 0::2] = words & 0xF
        nib[..., 1::2] = words >> 4
        vals = E2M1[nib]
    vals = vals * np.repeat(np.exp2(scales.astype(np.float64) - 127.0), 8, axis=1)[..., None]
    return vals.transpose(0, 1, 3, 2).reshape(g * 512, n)


def sgn(shape):
    return np.random.uniform(0.5, 2.0, shape) * np.where(np.random.standard_normal(shape) < 0, -1.0, 1.0)


K, J, R, T, F, S, O, N, Z, W = 512, 512, 512, 2048, 1024, 256, 128, 256, 1024, 512


def setup_inputs():
    n = np.random.standard_normal
    idx = np.stack([np.random.permutation(T)[:J] for _ in range(8)])
    idx2 = np.stack([np.random.permutation(T)[:J] for _ in range(8)])
    idx3 = np.random.permutation(F)[:R]
    idx4 = np.stack([np.random.permutation(J)[:S] for _ in range(8)])
    idx5 = np.random.permutation(J)[:S]
    idx6 = np.stack([np.random.permutation(Z)[:W] for _ in range(8)])
    idx7 = np.random.permutation(W)[:N]
    fk = mx_kscale(K)
    fr = mx_kscale(R)
    tr = np.ones(F)
    tr[idx3] = fr
    wtp = pack_weight(n((K, F)) * 1 / np.sqrt(K) / fk[:, None] * tr, "e4m3")
    return {
        "ta": (np.random.randint(-7, 8, (K, T)).astype(np.float64)).astype(np.float32),
        "ga": ((np.random.randint(10, 25, (K, 1)) / 64.0) * fk[:, None]).astype(np.float32),
        "gb": ((np.random.randint(4, 13, (K, 1)) / 64.0) * fk[:, None]).astype(np.float32),
        "wt_words": wtp[0],
        "wt_scales": wtp[1],
        "sa": (sgn((R, 1))).astype(np.float32),
        "sb": (sgn((R, 1))).astype(np.float32),
        "va": (np.random.randint(-7, 8, (R, Z)).astype(np.float64)).astype(np.float32),
        "ea": ((np.random.randint(8, 25, (R, 1)) / 1024.0) / fr[:, None]).astype(np.float32),
        "eb": (np.random.uniform(0.5, 1.6, (R, 1))).astype(np.float32),
        "offs": striped8(idx),
        "offs2": striped8(idx2),
        "offs3": striped(idx3),
        "offs4": striped8(idx4),
        "offs5": striped(idx5),
        "offs6": striped8(idx6),
        "offs7": striped(idx7),
    }


def reference(ta, ga, gb, wt_words, wt_scales, sa, sb, va, ea, eb, offs, offs2, offs3, offs4, offs5, offs6, offs7):
    idx = unstriped8(offs)
    idx2 = unstriped8(offs2)
    idx3 = unstriped(offs3)
    idx4 = unstriped8(offs4)
    idx5 = unstriped(offs5)
    idx6 = unstriped8(offs6)
    idx7 = unstriped(offs7)
    wtu = unpack_weight(wt_words, wt_scales, "e4m3")
    xc = pick8(f64(ta), idx, 64) * f64(ga) + pick8(f64(ta), idx2, 64) * f64(gb)
    wtidx3g = wtu[:, idx3]
    xcq = mxq(xc, 0, "e4m3")
    a = wtidx3g.T @ xcq
    h1 = np.maximum(pick8(a, idx4, 64) * f64(sa), a[:, idx5] * f64(sb))
    hid = h1.reshape(R, O, S // O).max(axis=2)
    vcd = pick8(f64(va), idx6, 64) * f64(ea)
    vc = vcd[:, idx7] * f64(eb)
    vcq = mxq(vc, 0, "e4m3")
    hidq = mxq(hid, 0, "e4m3")
    y = vcq.T @ hidq
    return y

@@ -1,0 +1,170 @@
+from contextlib import ExitStack
+
+import concourse.mybir as mybir
+
+K, J, R, T, F, S, O, N, Z, W = 512, 512, 512, 2048, 1024, 256, 128, 256, 1024, 512
+FLOPS = 2 * K * R * J + 2 * R * N * O
+
+F32 = mybir.dt.float32
+BF16 = mybir.dt.bfloat16
+I32 = mybir.dt.int32
+U32 = mybir.dt.uint32
+U16 = mybir.dt.uint16
+U8 = mybir.dt.uint8
+FP8X4 = mybir.dt.float8_e4m3fn_x4
+COPY = mybir.ActivationFunctionType.Copy
+ADD = mybir.AluOpType.add
+MAX = mybir.AluOpType.max
+XY = mybir.AxisListType.XY
+
+P = 128
+PACK = 4
+
+
+def tile_picked_refined_store_one_pooledgroups_respelled_plain_kernel(
+    tc, ta, ga, gb, wt_words, wt_scales, sa, sb, va, ea, eb, offs, offs2, offs3, offs4, offs5, offs6, offs7, out
+):
+    nc = tc.nc
+    with ExitStack() as ctx:
+        keep = ctx.enter_context(tc.tile_pool(name="keep", bufs=1))
+        psum = ctx.enter_context(tc.psum_pool(name="psum", bufs=1))
+
+        def load_list(src, name):
+            tile = keep.tile(list(src.shape), U16, name=name)
+            nc.sync.dma_start(tile[:], src)
+            return tile
+
+        def load_factor(queue, src, name):
+            tile = keep.tile([P, PACK], F32, name=name)
+            queue.dma_start(tile[:], src.rearrange("(p t) one -> p (t one)", t=PACK))
+            return tile
+
+        def load_rows(src, t, name):
+            tile = keep.tile([P, src.shape[1]], F32, name=name)
+            nc.sync.dma_start(tile[:], src.rearrange("(p t) c -> p t c", t=PACK)[:, t, :])
+            return tile
+
+        def fetch(dst, window, offsets, factor, t):
+            nc.scalar.activation(out=dst, in_=window[:].indirect(offsets[:]), func=COPY, scale=factor[:, t : t + 1])
+
+        va_sb = [None] * PACK
+        ta_sb = [None] * PACK
+        va_sb[0] = load_rows(va, 0, "va0")
+        ea_sb = load_factor(nc.scalar, ea, "ea_sb")
+        l6 = load_list(offs6, "l6")
+        eb_sb = load_factor(nc.scalar, eb, "eb_sb")
+        l7 = load_list(offs7, "l7")
+        ga_sb = load_factor(nc.scalar, ga, "ga_sb")
+        ta_sb[0] = load_rows(ta, 0, "ta0")
+        gb_sb = load_factor(nc.scalar, gb, "gb_sb")
+        l1 = load_list(offs, "l1")
+        l2 = load_list(offs2, "l2")
+        ta_sb[1] = load_rows(ta, 1, "ta1")
+        l3 = load_list(offs3, "l3")
+        for t in range(2, PACK):
+            ta_sb[t] = load_rows(ta, t, f"ta{t}")
+        words = keep.tile([P, F], I32, name="words")
+        nc.sync.dma_start(words[:], wt_words[0].rearrange("p c t -> p (c t)").bitcast(I32))
+        for t in range(1, PACK):
+            va_sb[t] = load_rows(va, t, f"va{t}")
+        l4 = load_list(offs4, "l4")
+        l5 = load_list(offs5, "l5")
+
+        staged = keep.tile([4, 4, F // 4], I32, name="staged")
+        nc.gpsimd.dma_start(staged[:], wt_scales[0].bitcast(I32).rearrange("(q i) c -> i q c", i=4))
+        plane = keep.tile([P, F], U8, name="plane")
+        nc.vector.memset(plane[:].bitcast(I32), 0)
+        for q in range(4):
+            nc.vector.tensor_copy(plane[32 * q : 32 * q + 4, :].bitcast(I32), staged[:, q, :])
+        sa_sb = load_factor(nc.gpsimd, sa, "sa_sb")
+        sb_sb = load_factor(nc.gpsimd, sb, "sb_sb")
+
+        vc_planes = keep.tile([P, PACK, N], BF16, name="vc_planes")
+
+        def spell(t):
+            vcd = keep.tile([P, W], F32, name=f"vcd{t}")
+            fetch(vcd[:], va_sb[t], l6, ea_sb, t)
+            fetch(vc_planes[:, t, :], vcd, l7, eb_sb, t)
+
+        spell(0)
+
+        xc_planes = keep.tile([P, PACK, J], BF16, name="xc_planes")
+        for t in range(PACK):
+            coarse = keep.tile([P, J], F32, name=f"coarse{t}")
+            fine = keep.tile([P, J], F32, name=f"fine{t}")
+            fetch(coarse[:], ta_sb[t], l1, ga_sb, t)
+            fetch(fine[:], ta_sb[t], l2, gb_sb, t)
+            nc.vector.tensor_tensor(xc_planes[:, t, :], coarse[:], fine[:], ADD)
+
+        wt_codes = keep.tile([P, R], U32, name="wt_codes", align_bytes=64)
+        wt_bytes = keep.tile([P, R], U8, name="wt_bytes", align_bytes=64)
+        nc.vector.tensor_copy(wt_bytes[:].rearrange("p (t m) -> p m t", t=PACK), plane[:].indirect(l3[:]))
+        nc.vector.tensor_copy(
+            wt_codes[:].rearrange("p (t m) -> p m t", t=PACK), words[:].bitcast(U32).indirect(l3[:])
+        )
+
+        def quantise(grouped, width, name):
+            codes = keep.tile([P, width], U32, name=name + "_codes", align_bytes=64)
+            scale = keep.tile([P, width], U8, name=name + "_scale", align_bytes=64)
+            nc.vector.quantize_mx(
+                out=codes[:].bitcast(FP8X4), scales=scale[:], in_=grouped[:].rearrange("p c t -> p (c t)")
+            )
+            return codes, scale
+
+        xc_grouped = keep.tile([P, J, PACK], BF16, name="xc_grouped", align_bytes=64)
+        nc.vector.tensor_copy(xc_grouped[:], xc_planes[:].rearrange("p t j -> p j t"))
+        xc_codes, xc_scale = quantise(xc_grouped, J, "xc")
+
+        for t in range(1, PACK):
+            spell(t)
+
+        a_sb = []
+        for t in range(PACK):
+            cols = slice(t * P, (t + 1) * P)
+            bank = psum.tile([P, J], F32, name=f"a_bank{t}")
+            nc.tensor.matmul_mx(
+                out=bank[:],
+                lhsT=wt_codes[:, cols].bitcast(FP8X4),
+                lhsT_scale=wt_bytes[:, cols],
+                rhs=xc_codes[:].bitcast(FP8X4),
+                rhs_scale=xc_scale[:],
+                start=True,
+                stop=True,
+            )
+            rows = keep.tile([P, J], F32, name=f"a{t}")
+            nc.vector.tensor_copy(rows[:], bank[:])
+            a_sb.append(rows)
+
+        vc_grouped = keep.tile([P, N, PACK], BF16, name="vc_grouped", align_bytes=64)
+        nc.vector.tensor_copy(vc_grouped[:], vc_planes[:].rearrange("p t n -> p n t"))
+        vc_codes, vc_scale = quantise(vc_grouped, N, "vc")
+
+        hid_grouped = keep.tile([P, O, PACK], BF16, name="hid_grouped", align_bytes=64)
+        for t in range(PACK):
+            picks = keep.tile([P, 2, S], F32, name=f"picks{t}")
+            fetch(picks[:, 0, :], a_sb[t], l4, sa_sb, t)
+            fetch(picks[:, 1, :], a_sb[t], l5, sb_sb, t)
+            nc.vector.tensor_reduce(
+                out=hid_grouped[:, :, t], in_=picks[:].rearrange("p a (o e) -> p o a e", e=S // O), axis=XY, op=MAX
+            )
+        hid_codes, hid_scale = quantise(hid_grouped, O, "hid")
+
+        for c in range(N // P):
+            cols = slice(c * P, (c + 1) * P)
+            bank = psum.tile([P, O], F32, name=f"y_bank{c}")
+            nc.tensor.matmul_mx(
+                out=bank[:],
+                lhsT=vc_codes[:, cols].bitcast(FP8X4),
+                lhsT_scale=vc_scale[:, cols],
+                rhs=hid_codes[:].bitcast(FP8X4),
+                rhs_scale=hid_scale[:],
+                start=True,
+                stop=True,
+            )
+            result = keep.tile([P, O], F32, name=f"y{c}")
+            if c == 0:
+                nc.vector.tensor_copy(result[:], bank[:])
+                nc.sync.dma_start(out[cols, :], result[:])
+            else:
+                nc.scalar.copy(result[:], bank[:])
+                nc.scalar.dma_start(out[cols, :], result[:])

@@ -19,6 +19,7 @@ XY = mybir.AxisListType.XY
 
 P = 128
 PACK = 4
+HALF = J // 2
 
 
 def tile_picked_refined_store_one_pooledgroups_respelled_plain_kernel(
@@ -45,56 +46,80 @@ def tile_picked_refined_store_one_pooledgroups_respelled_plain_kernel(
             return tile
 
         def fetch(dst, window, offsets, factor, t):
-            nc.scalar.activation(out=dst, in_=window[:].indirect(offsets[:]), func=COPY, scale=factor[:, t : t + 1])
+            nc.scalar.activation(out=dst, in_=window[:].indirect(offsets), func=COPY, scale=factor[:, t : t + 1])
 
         va_sb = [None] * PACK
         ta_sb = [None] * PACK
-        va_sb[0] = load_rows(va, 0, "va0")
-        ea_sb = load_factor(nc.scalar, ea, "ea_sb")
         l6 = load_list(offs6, "l6")
+        ea_sb = load_factor(nc.scalar, ea, "ea_sb")
+        va_sb[0] = load_rows(va, 0, "va0")
         eb_sb = load_factor(nc.scalar, eb, "eb_sb")
         l7 = load_list(offs7, "l7")
         ga_sb = load_factor(nc.scalar, ga, "ga_sb")
-        ta_sb[0] = load_rows(ta, 0, "ta0")
-        gb_sb = load_factor(nc.scalar, gb, "gb_sb")
         l1 = load_list(offs, "l1")
+        ta_sb[0] = load_rows(ta, 0, "ta0")
         l2 = load_list(offs2, "l2")
         ta_sb[1] = load_rows(ta, 1, "ta1")
         l3 = load_list(offs3, "l3")
         for t in range(2, PACK):
             ta_sb[t] = load_rows(ta, t, f"ta{t}")
-        words = keep.tile([P, F], I32, name="words")
+        words = keep.tile([P, F], I32, name="words", tag="reused")
         nc.sync.dma_start(words[:], wt_words[0].rearrange("p c t -> p (c t)").bitcast(I32))
         for t in range(1, PACK):
             va_sb[t] = load_rows(va, t, f"va{t}")
         l4 = load_list(offs4, "l4")
         l5 = load_list(offs5, "l5")
+        sa_sb = load_factor(nc.sync, sa, "sa_sb")
+        sb_sb = load_factor(nc.sync, sb, "sb_sb")
 
+        gb_sb = load_factor(nc.gpsimd, gb, "gb_sb")
         staged = keep.tile([4, 4, F // 4], I32, name="staged")
         nc.gpsimd.dma_start(staged[:], wt_scales[0].bitcast(I32).rearrange("(q i) c -> i q c", i=4))
         plane = keep.tile([P, F], U8, name="plane")
         nc.vector.memset(plane[:].bitcast(I32), 0)
         for q in range(4):
             nc.vector.tensor_copy(plane[32 * q : 32 * q + 4, :].bitcast(I32), staged[:, q, :])
-        sa_sb = load_factor(nc.gpsimd, sa, "sa_sb")
-        sb_sb = load_factor(nc.gpsimd, sb, "sb_sb")
 
-        vc_planes = keep.tile([P, PACK, N], BF16, name="vc_planes")
+        warm_in = keep.tile([P, 1], F32, name="warm_in")
+        warm_out = keep.tile([P, 1], F32, name="warm_out")
+        nc.vector.memset(warm_in[:], 0.0)
+        nc.scalar.activation(out=warm_out[:], in_=warm_in[:], func=COPY)
+
+        vc_pairs = [keep.tile([P, 2, N], BF16, name=f"vc_pair{u}") for u in range(2)]
+        vc_grouped = keep.tile([P, N, PACK], BF16, name="vc_grouped", align_bytes=64)
 
         def spell(t):
             vcd = keep.tile([P, W], F32, name=f"vcd{t}")
-            fetch(vcd[:], va_sb[t], l6, ea_sb, t)
-            fetch(vc_planes[:, t, :], vcd, l7, eb_sb, t)
+            fetch(vcd[:], va_sb[t], l6[:], ea_sb, t)
+            fetch(vc_pairs[t // 2][:, t % 2, :], vcd, l7[:], eb_sb, t)
+
+        def weave_vc(u):
+            nc.vector.tensor_copy(vc_grouped[:, :, 2 * u : 2 * u + 2], vc_pairs[u][:].rearrange("p e n -> p n e"))
 
         spell(0)
 
-        xc_planes = keep.tile([P, PACK, J], BF16, name="xc_planes")
-        for t in range(PACK):
+        xc_grouped = keep.tile([P, J, PACK], BF16, name="xc_grouped", align_bytes=64)
+
+        def sum_codes(t, planes):
             coarse = keep.tile([P, J], F32, name=f"coarse{t}")
             fine = keep.tile([P, J], F32, name=f"fine{t}")
-            fetch(coarse[:], ta_sb[t], l1, ga_sb, t)
-            fetch(fine[:], ta_sb[t], l2, gb_sb, t)
-            nc.vector.tensor_tensor(xc_planes[:, t, :], coarse[:], fine[:], ADD)
+            fetch(coarse[:], ta_sb[t], l1[:], ga_sb, t)
+            fetch(fine[:], ta_sb[t], l2[:], gb_sb, t)
+            for h in range(2):
+                cols = slice(h * HALF, (h + 1) * HALF)
+                nc.vector.tensor_tensor(planes[:, h, t % 2, :], coarse[:, cols], fine[:, cols], ADD)
+
+        def weave(u, planes):
+            for h in range(2):
+                cols = slice(h * HALF, (h + 1) * HALF)
+                nc.vector.tensor_copy(
+                    xc_grouped[:, cols, 2 * u : 2 * u + 2], planes[:, h, :, :].rearrange("p e j -> p j e")
+                )
+
+        low = keep.tile([P, 2, 2, HALF], BF16, name="xc_low")
+        sum_codes(0, low)
+        sum_codes(1, low)
+        weave(0, low)
 
         wt_codes = keep.tile([P, R], U32, name="wt_codes", align_bytes=64)
         wt_bytes = keep.tile([P, R], U8, name="wt_bytes", align_bytes=64)
@@ -103,17 +128,23 @@ def tile_picked_refined_store_one_pooledgroups_respelled_plain_kernel(
             wt_codes[:].rearrange("p (t m) -> p m t", t=PACK), words[:].bitcast(U32).indirect(l3[:])
         )
 
-        def quantise(grouped, width, name):
+        def quantise(grouped, width, pieces, name):
             codes = keep.tile([P, width], U32, name=name + "_codes", align_bytes=64)
             scale = keep.tile([P, width], U8, name=name + "_scale", align_bytes=64)
-            nc.vector.quantize_mx(
-                out=codes[:].bitcast(FP8X4), scales=scale[:], in_=grouped[:].rearrange("p c t -> p (c t)")
-            )
+            for i in range(pieces):
+                cols = slice(i * width // pieces, (i + 1) * width // pieces)
+                nc.vector.quantize_mx(
+                    out=codes[:, cols].bitcast(FP8X4),
+                    scales=scale[:, cols],
+                    in_=grouped[:, cols, :].rearrange("p c t -> p (c t)"),
+                )
             return codes, scale
 
-        xc_grouped = keep.tile([P, J, PACK], BF16, name="xc_grouped", align_bytes=64)
-        nc.vector.tensor_copy(xc_grouped[:], xc_planes[:].rearrange("p t j -> p j t"))
-        xc_codes, xc_scale = quantise(xc_grouped, J, "xc")
+        high = keep.tile([P, 2, 2, HALF], BF16, name="xc_high", tag="reused")
+        sum_codes(2, high)
+        sum_codes(3, high)
+        weave(1, high)
+        xc_codes, xc_scale = quantise(xc_grouped, J, 2, "xc")
 
         for t in range(1, PACK):
             spell(t)
@@ -135,19 +166,25 @@ def tile_picked_refined_store_one_pooledgroups_respelled_plain_kernel(
             nc.vector.tensor_copy(rows[:], bank[:])
             a_sb.append(rows)
 
-        vc_grouped = keep.tile([P, N, PACK], BF16, name="vc_grouped", align_bytes=64)
-        nc.vector.tensor_copy(vc_grouped[:], vc_planes[:].rearrange("p t n -> p n t"))
-        vc_codes, vc_scale = quantise(vc_grouped, N, "vc")
+        weave_vc(0)
+        weave_vc(1)
+        vc_codes, vc_scale = quantise(vc_grouped, N, 1, "vc")
 
         hid_grouped = keep.tile([P, O, PACK], BF16, name="hid_grouped", align_bytes=64)
         for t in range(PACK):
             picks = keep.tile([P, 2, S], F32, name=f"picks{t}")
-            fetch(picks[:, 0, :], a_sb[t], l4, sa_sb, t)
-            fetch(picks[:, 1, :], a_sb[t], l5, sb_sb, t)
-            nc.vector.tensor_reduce(
-                out=hid_grouped[:, :, t], in_=picks[:].rearrange("p a (o e) -> p o a e", e=S // O), axis=XY, op=MAX
-            )
-        hid_codes, hid_scale = quantise(hid_grouped, O, "hid")
+            fetch(picks[:, 1, :], a_sb[t], l5[:], sb_sb, t)
+            pieces = 2 if t == PACK - 1 else 1
+            for i in range(pieces):
+                n = S // pieces
+                fetch(picks[:, 0, i * n : (i + 1) * n], a_sb[t], l4[:, i * n // 16 : (i + 1) * n // 16], sa_sb, t)
+                nc.vector.tensor_reduce(
+                    out=hid_grouped[:, i * n // 2 : (i + 1) * n // 2, t],
+                    in_=picks[:, :, i * n : (i + 1) * n].rearrange("p a (o e) -> p o a e", e=S // O),
+                    axis=XY,
+                    op=MAX,
+                )
+        hid_codes, hid_scale = quantise(hid_grouped, O, 1, "hid")
 
         for c in range(N // P):
             cols = slice(c * P, (c + 1) * P)

@@ -50,22 +50,23 @@ def tile_picked_refined_store_one_pooledgroups_respelled_plain_kernel(
 
         va_sb = [None] * PACK
         ta_sb = [None] * PACK
-        l6 = load_list(offs6, "l6")
-        ea_sb = load_factor(nc.scalar, ea, "ea_sb")
         va_sb[0] = load_rows(va, 0, "va0")
+        ea_sb = load_factor(nc.scalar, ea, "ea_sb")
+        l6 = load_list(offs6, "l6")
         eb_sb = load_factor(nc.scalar, eb, "eb_sb")
         l7 = load_list(offs7, "l7")
-        ga_sb = load_factor(nc.scalar, ga, "ga_sb")
+        va_sb[1] = load_rows(va, 1, "va1")
         l1 = load_list(offs, "l1")
         ta_sb[0] = load_rows(ta, 0, "ta0")
+        ga_sb = load_factor(nc.sync, ga, "ga_sb")
         l2 = load_list(offs2, "l2")
         ta_sb[1] = load_rows(ta, 1, "ta1")
         l3 = load_list(offs3, "l3")
         for t in range(2, PACK):
             ta_sb[t] = load_rows(ta, t, f"ta{t}")
-        words = keep.tile([P, F], I32, name="words", tag="reused")
+        words = keep.tile([P, F], I32, name="words")
         nc.sync.dma_start(words[:], wt_words[0].rearrange("p c t -> p (c t)").bitcast(I32))
-        for t in range(1, PACK):
+        for t in range(2, PACK):
             va_sb[t] = load_rows(va, t, f"va{t}")
         l4 = load_list(offs4, "l4")
         l5 = load_list(offs5, "l5")
@@ -97,6 +98,8 @@ def tile_picked_refined_store_one_pooledgroups_respelled_plain_kernel(
             nc.vector.tensor_copy(vc_grouped[:, :, 2 * u : 2 * u + 2], vc_pairs[u][:].rearrange("p e n -> p n e"))
 
         spell(0)
+        spell(1)
+        weave_vc(0)
 
         xc_grouped = keep.tile([P, J, PACK], BF16, name="xc_grouped", align_bytes=64)
 
@@ -140,33 +143,35 @@ def tile_picked_refined_store_one_pooledgroups_respelled_plain_kernel(
                 )
             return codes, scale
 
-        high = keep.tile([P, 2, 2, HALF], BF16, name="xc_high", tag="reused")
+        high = keep.tile([P, 2, 2, HALF], BF16, name="xc_high")
         sum_codes(2, high)
         sum_codes(3, high)
         weave(1, high)
         xc_codes, xc_scale = quantise(xc_grouped, J, 2, "xc")
 
-        for t in range(1, PACK):
-            spell(t)
+        spell(2)
+        spell(3)
 
         a_sb = []
         for t in range(PACK):
             cols = slice(t * P, (t + 1) * P)
-            bank = psum.tile([P, J], F32, name=f"a_bank{t}")
-            nc.tensor.matmul_mx(
-                out=bank[:],
-                lhsT=wt_codes[:, cols].bitcast(FP8X4),
-                lhsT_scale=wt_bytes[:, cols],
-                rhs=xc_codes[:].bitcast(FP8X4),
-                rhs_scale=xc_scale[:],
-                start=True,
-                stop=True,
-            )
             rows = keep.tile([P, J], F32, name=f"a{t}")
-            nc.vector.tensor_copy(rows[:], bank[:])
+            pieces = 2 if t == 0 else 1
+            for i in range(pieces):
+                slots = slice(i * J // pieces, (i + 1) * J // pieces)
+                bank = psum.tile([P, J // pieces], F32, name=f"a_bank{t}_{i}")
+                nc.tensor.matmul_mx(
+                    out=bank[:],
+                    lhsT=wt_codes[:, cols].bitcast(FP8X4),
+                    lhsT_scale=wt_bytes[:, cols],
+                    rhs=xc_codes[:, slots].bitcast(FP8X4),
+                    rhs_scale=xc_scale[:, slots],
+                    start=True,
+                    stop=True,
+                )
+                nc.vector.tensor_copy(rows[:, slots], bank[:])
             a_sb.append(rows)
 
-        weave_vc(0)
         weave_vc(1)
         vc_codes, vc_scale = quantise(vc_grouped, N, 1, "vc")
 

@@ -35,9 +35,9 @@ def tile_picked_refined_store_one_pooledgroups_respelled_plain_kernel(
             nc.sync.dma_start(tile[:], src)
             return tile
 
-        def load_factor(queue, src, name):
-            tile = keep.tile([P, PACK], F32, name=name)
-            queue.dma_start(tile[:], src.rearrange("(p t) one -> p (t one)", t=PACK))
+        def load_factor(queue, src, name, first=0, last=PACK):
+            tile = keep.tile([P, last - first], F32, name=name)
+            queue.dma_start(tile[:], src.rearrange("(p t) one -> p (t one)", t=PACK)[:, first:last])
             return tile
 
         def load_rows(src, t, name):
@@ -53,9 +53,9 @@ def tile_picked_refined_store_one_pooledgroups_respelled_plain_kernel(
         va_sb[0] = load_rows(va, 0, "va0")
         ea_sb = load_factor(nc.scalar, ea, "ea_sb")
         l6 = load_list(offs6, "l6")
-        eb_sb = load_factor(nc.scalar, eb, "eb_sb")
-        l7 = load_list(offs7, "l7")
+        eb_sb = [load_factor(nc.scalar, eb, "eb_low", 0, 2)]
         va_sb[1] = load_rows(va, 1, "va1")
+        l7 = load_list(offs7, "l7")
         l1 = load_list(offs, "l1")
         ta_sb[0] = load_rows(ta, 0, "ta0")
         ga_sb = load_factor(nc.sync, ga, "ga_sb")
@@ -68,6 +68,7 @@ def tile_picked_refined_store_one_pooledgroups_respelled_plain_kernel(
         nc.sync.dma_start(words[:], wt_words[0].rearrange("p c t -> p (c t)").bitcast(I32))
         for t in range(2, PACK):
             va_sb[t] = load_rows(va, t, f"va{t}")
+        eb_sb.append(load_factor(nc.sync, eb, "eb_high", 2, 4))
         l4 = load_list(offs4, "l4")
         l5 = load_list(offs5, "l5")
         sa_sb = load_factor(nc.sync, sa, "sa_sb")
@@ -89,16 +90,19 @@ def tile_picked_refined_store_one_pooledgroups_respelled_plain_kernel(
         vc_pairs = [keep.tile([P, 2, N], BF16, name=f"vc_pair{u}") for u in range(2)]
         vc_grouped = keep.tile([P, N, PACK], BF16, name="vc_grouped", align_bytes=64)
 
-        def spell(t):
-            vcd = keep.tile([P, W], F32, name=f"vcd{t}")
-            fetch(vcd[:], va_sb[t], l6[:], ea_sb, t)
-            fetch(vc_pairs[t // 2][:, t % 2, :], vcd, l7[:], eb_sb, t)
+        def spell(u):
+            words_of = []
+            for t in (2 * u, 2 * u + 1):
+                vcd = keep.tile([P, W], F32, name=f"vcd{t}")
+                fetch(vcd[:], va_sb[t], l6[:], ea_sb, t)
+                words_of.append(vcd)
+            for e in range(2):
+                fetch(vc_pairs[u][:, e, :], words_of[e], l7[:], eb_sb[u], e)
 
         def weave_vc(u):
             nc.vector.tensor_copy(vc_grouped[:, :, 2 * u : 2 * u + 2], vc_pairs[u][:].rearrange("p e n -> p n e"))
 
         spell(0)
-        spell(1)
         weave_vc(0)
 
         xc_grouped = keep.tile([P, J, PACK], BF16, name="xc_grouped", align_bytes=64)
@@ -149,8 +153,7 @@ def tile_picked_refined_store_one_pooledgroups_respelled_plain_kernel(
         weave(1, high)
         xc_codes, xc_scale = quantise(xc_grouped, J, 2, "xc")
 
-        spell(2)
-        spell(3)
+        spell(1)
 
         a_sb = []
         for t in range(PACK):

from contextlib import ExitStack

import concourse.mybir as mybir

K, J, R, T, F, S, O, N, Z, W = 512, 512, 512, 2048, 1024, 256, 128, 256, 1024, 512
FLOPS = 2 * K * R * J + 2 * R * N * O

F32 = mybir.dt.float32
BF16 = mybir.dt.bfloat16
I32 = mybir.dt.int32
U32 = mybir.dt.uint32
U16 = mybir.dt.uint16
U8 = mybir.dt.uint8
FP8X4 = mybir.dt.float8_e4m3fn_x4
COPY = mybir.ActivationFunctionType.Copy
ADD = mybir.AluOpType.add
MAX = mybir.AluOpType.max
XY = mybir.AxisListType.XY

P = 128
PACK = 4
HALF = J // 2


def tile_picked_refined_store_one_pooledgroups_respelled_plain_kernel(
    tc, ta, ga, gb, wt_words, wt_scales, sa, sb, va, ea, eb, offs, offs2, offs3, offs4, offs5, offs6, offs7, out
):
    nc = tc.nc
    with ExitStack() as ctx:
        keep = ctx.enter_context(tc.tile_pool(name="keep", bufs=1))
        psum = ctx.enter_context(tc.psum_pool(name="psum", bufs=1))

        def load_list(src, name):
            tile = keep.tile(list(src.shape), U16, name=name)
            nc.sync.dma_start(tile[:], src)
            return tile

        def load_factor(queue, src, name, first=0, last=PACK):
            tile = keep.tile([P, last - first], F32, name=name)
            queue.dma_start(tile[:], src.rearrange("(p t) one -> p (t one)", t=PACK)[:, first:last])
            return tile

        def load_rows(src, t, name):
            tile = keep.tile([P, src.shape[1]], F32, name=name)
            nc.sync.dma_start(tile[:], src.rearrange("(p t) c -> p t c", t=PACK)[:, t, :])
            return tile

        def fetch(dst, window, offsets, factor, t):
            nc.scalar.activation(out=dst, in_=window[:].indirect(offsets), func=COPY, scale=factor[:, t : t + 1])

        va_sb = [None] * PACK
        ta_sb = [None] * PACK
        va_sb[0] = load_rows(va, 0, "va0")
        ea_sb = load_factor(nc.scalar, ea, "ea_sb")
        l6 = load_list(offs6, "l6")
        eb_sb = [load_factor(nc.scalar, eb, "eb_low", 0, 2)]
        va_sb[1] = load_rows(va, 1, "va1")
        l7 = load_list(offs7, "l7")
        l1 = load_list(offs, "l1")
        ta_sb[0] = load_rows(ta, 0, "ta0")
        ga_sb = load_factor(nc.sync, ga, "ga_sb")
        l2 = load_list(offs2, "l2")
        ta_sb[1] = load_rows(ta, 1, "ta1")
        l3 = load_list(offs3, "l3")
        for t in range(2, PACK):
            ta_sb[t] = load_rows(ta, t, f"ta{t}")
        words = keep.tile([P, F], I32, name="words")
        nc.sync.dma_start(words[:], wt_words[0].rearrange("p c t -> p (c t)").bitcast(I32))
        for t in range(2, PACK):
            va_sb[t] = load_rows(va, t, f"va{t}")
        eb_sb.append(load_factor(nc.sync, eb, "eb_high", 2, 4))
        l4 = load_list(offs4, "l4")
        l5 = load_list(offs5, "l5")
        sa_sb = load_factor(nc.sync, sa, "sa_sb")
        sb_sb = load_factor(nc.sync, sb, "sb_sb")

        gb_sb = load_factor(nc.gpsimd, gb, "gb_sb")
        staged = keep.tile([4, 4, F // 4], I32, name="staged")
        nc.gpsimd.dma_start(staged[:], wt_scales[0].bitcast(I32).rearrange("(q i) c -> i q c", i=4))
        plane = keep.tile([P, F], U8, name="plane")
        nc.vector.memset(plane[:].bitcast(I32), 0)
        for q in range(4):
            nc.vector.tensor_copy(plane[32 * q : 32 * q + 4, :].bitcast(I32), staged[:, q, :])

        warm_in = keep.tile([P, 1], F32, name="warm_in")
        warm_out = keep.tile([P, 1], F32, name="warm_out")
        nc.vector.memset(warm_in[:], 0.0)
        nc.scalar.activation(out=warm_out[:], in_=warm_in[:], func=COPY)

        vc_pairs = [keep.tile([P, 2, N], BF16, name=f"vc_pair{u}") for u in range(2)]
        vc_grouped = keep.tile([P, N, PACK], BF16, name="vc_grouped", align_bytes=64)

        def spell(u):
            words_of = []
            for t in (2 * u, 2 * u + 1):
                vcd = keep.tile([P, W], F32, name=f"vcd{t}")
                fetch(vcd[:], va_sb[t], l6[:], ea_sb, t)
                words_of.append(vcd)
            for e in range(2):
                fetch(vc_pairs[u][:, e, :], words_of[e], l7[:], eb_sb[u], e)

        def weave_vc(u):
            nc.vector.tensor_copy(vc_grouped[:, :, 2 * u : 2 * u + 2], vc_pairs[u][:].rearrange("p e n -> p n e"))

        spell(0)
        weave_vc(0)

        xc_grouped = keep.tile([P, J, PACK], BF16, name="xc_grouped", align_bytes=64)

        def sum_codes(t, planes):
            coarse = keep.tile([P, J], F32, name=f"coarse{t}")
            fine = keep.tile([P, J], F32, name=f"fine{t}")
            fetch(coarse[:], ta_sb[t], l1[:], ga_sb, t)
            fetch(fine[:], ta_sb[t], l2[:], gb_sb, t)
            for h in range(2):
                cols = slice(h * HALF, (h + 1) * HALF)
                nc.vector.tensor_tensor(planes[:, h, t % 2, :], coarse[:, cols], fine[:, cols], ADD)

        def weave(u, planes):
            for h in range(2):
                cols = slice(h * HALF, (h + 1) * HALF)
                nc.vector.tensor_copy(
                    xc_grouped[:, cols, 2 * u : 2 * u + 2], planes[:, h, :, :].rearrange("p e j -> p j e")
                )

        low = keep.tile([P, 2, 2, HALF], BF16, name="xc_low")
        sum_codes(0, low)
        sum_codes(1, low)
        weave(0, low)

        wt_codes = keep.tile([P, R], U32, name="wt_codes", align_bytes=64)
        wt_bytes = keep.tile([P, R], U8, name="wt_bytes", align_bytes=64)
        nc.vector.tensor_copy(wt_bytes[:].rearrange("p (t m) -> p m t", t=PACK), plane[:].indirect(l3[:]))
        nc.vector.tensor_copy(
            wt_codes[:].rearrange("p (t m) -> p m t", t=PACK), words[:].bitcast(U32).indirect(l3[:])
        )

        def quantise(grouped, width, pieces, name):
            codes = keep.tile([P, width], U32, name=name + "_codes", align_bytes=64)
            scale = keep.tile([P, width], U8, name=name + "_scale", align_bytes=64)
            for i in range(pieces):
                cols = slice(i * width // pieces, (i + 1) * width // pieces)
                nc.vector.quantize_mx(
                    out=codes[:, cols].bitcast(FP8X4),
                    scales=scale[:, cols],
                    in_=grouped[:, cols, :].rearrange("p c t -> p (c t)"),
                )
            return codes, scale

        high = keep.tile([P, 2, 2, HALF], BF16, name="xc_high")
        sum_codes(2, high)
        sum_codes(3, high)
        weave(1, high)
        xc_codes, xc_scale = quantise(xc_grouped, J, 2, "xc")

        spell(1)

        a_sb = []
        for t in range(PACK):
            cols = slice(t * P, (t + 1) * P)
            rows = keep.tile([P, J], F32, name=f"a{t}")
            pieces = 2 if t == 0 else 1
            for i in range(pieces):
                slots = slice(i * J // pieces, (i + 1) * J // pieces)
                bank = psum.tile([P, J // pieces], F32, name=f"a_bank{t}_{i}")
                nc.tensor.matmul_mx(
                    out=bank[:],
                    lhsT=wt_codes[:, cols].bitcast(FP8X4),
                    lhsT_scale=wt_bytes[:, cols],
                    rhs=xc_codes[:, slots].bitcast(FP8X4),
                    rhs_scale=xc_scale[:, slots],
                    start=True,
                    stop=True,
                )
                nc.vector.tensor_copy(rows[:, slots], bank[:])
            a_sb.append(rows)

        weave_vc(1)
        vc_codes, vc_scale = quantise(vc_grouped, N, 1, "vc")

        hid_grouped = keep.tile([P, O, PACK], BF16, name="hid_grouped", align_bytes=64)
        for t in range(PACK):
            picks = keep.tile([P, 2, S], F32, name=f"picks{t}")
            fetch(picks[:, 1, :], a_sb[t], l5[:], sb_sb, t)
            pieces = 2 if t == PACK - 1 else 1
            for i in range(pieces):
                n = S // pieces
                fetch(picks[:, 0, i * n : (i + 1) * n], a_sb[t], l4[:, i * n // 16 : (i + 1) * n // 16], sa_sb, t)
                nc.vector.tensor_reduce(
                    out=hid_grouped[:, i * n // 2 : (i + 1) * n // 2, t],
                    in_=picks[:, :, i * n : (i + 1) * n].rearrange("p a (o e) -> p o a e", e=S // O),
                    axis=XY,
                    op=MAX,
                )
        hid_codes, hid_scale = quantise(hid_grouped, O, 1, "hid")

        for c in range(N // P):
            cols = slice(c * P, (c + 1) * P)
            bank = psum.tile([P, O], F32, name=f"y_bank{c}")
            nc.tensor.matmul_mx(
                out=bank[:],
                lhsT=vc_codes[:, cols].bitcast(FP8X4),
                lhsT_scale=vc_scale[:, cols],
                rhs=hid_codes[:].bitcast(FP8X4),
                rhs_scale=hid_scale[:],
                start=True,
                stop=True,
            )
            result = keep.tile([P, O], F32, name=f"y{c}")
            if c == 0:
                nc.vector.tensor_copy(result[:], bank[:])
                nc.sync.dma_start(out[cols, :], result[:])
            else:
                nc.scalar.copy(result[:], bank[:])
                nc.scalar.dma_start(out[cols, :], result[:])
